import numpy as np
import ml_dtypes


def mxq(x, axis, fmt="e4m3"):
    dtype, down = {"e4m3": (ml_dtypes.float8_e4m3fn, 7), "e5m2": (ml_dtypes.float8_e5m2, 14)}[fmt]
    v = np.moveaxis(np.asarray(x, np.float32).astype(ml_dtypes.bfloat16).astype(np.float64), axis, -1)
    blocks = v.reshape(v.shape[:-1] + (-1, 32))
    amax = np.abs(blocks).max(-1, keepdims=True)
    byte = np.maximum(np.where(amax > 0, np.frexp(amax)[1] - 1 + 127, 0) - down, 1)
    scale = np.exp2(byte - 127.0)
    codes = (blocks / scale).astype(np.float32).astype(dtype).astype(np.float64)
    return np.moveaxis((codes * scale).reshape(v.shape), -1, axis)


WIDE = False


def mx_kscale(k):
    if not WIDE:
        return np.ones(k)
    levels = np.array([10, -10, 5, -5, 0])
    if k % 512:
        return np.exp2(np.random.permutation(np.resize(levels, k // 32))).repeat(32)
    a = np.empty((k // 512, 16))
    for p in range(k // 512):
        a[p, :8] = np.random.permutation(np.resize(levels, 8))
        for g in range(8):
            far = levels[np.abs(levels - a[p, g]) >= 10]
            a[p, g + 8] = far[np.random.randint(len(far))]
    return np.exp2(a.ravel()).repeat(32)


def f64(x):
    return np.asarray(x).astype(np.float64)


def striped(idx):
    return np.tile(np.asarray(idx).reshape(-1, 16).T, (8, 1)).astype(np.uint16)


def unstriped(offs):
    return offs[:16].T.reshape(-1).astype(np.int64)


def sigmoid(v):
    return 1.0 / (1.0 + np.exp(-v))


D, T, I, Q = 512, 1024, 512, 256


def setup_inputs():
    n = np.random.standard_normal
    idx = np.random.permutation(T)[:I]
    idx2 = np.random.permutation(T)[:I]
    fd = mx_kscale(D)
    return {
        "query": (n((D, Q)) * 0.8 / np.sqrt(D) * fd[:, None]).astype(np.float32),
        "keys": (n((D, T)) + 0.7 * n((D, 1))).astype(np.float32),
        "steep": (np.random.uniform(4.0, 12.0, (I, 1))).astype(np.float32),
        "th": (np.random.uniform(0.3, 0.7, (I, 1))).astype(np.float32),
        "dsc": (np.random.uniform(0.5, 2.0, (1, D)) / fd).astype(np.float32),
        "offs": striped(idx),
        "offs2": striped(idx2),
    }


def reference(query, keys, steep, th, dsc, offs, offs2):
    idx = unstriped(offs)
    idx2 = unstriped(offs2)
    ka = f64(keys)[:, idx].T
    kb = f64(keys)[:, idx2].T
    al = sigmoid((np.mean(ka * kb, axis=1, keepdims=True) - f64(th)) * f64(steep)) * 0.5
    kj = (ka + (kb - ka) * al) * f64(dsc)
    km = kj.T
    queryq = mxq(f64(query), 0, "e4m3")
    kmq = mxq(km, 0, "e4m3")
    a = queryq.T @ kmq
    p = np.exp(a - np.max(a, axis=1, keepdims=True))
    y = p / np.sum(p, axis=1, keepdims=True) * 512.0
    return y

@@ -1,0 +1,233 @@
+from contextlib import ExitStack
+
+import concourse.mybir as mybir
+from concourse.masks import make_identity
+
+D, T, I, Q = 512, 1024, 512, 256
+FLOPS = 2 * D * I * Q
+
+F32 = mybir.dt.float32
+BF16 = mybir.dt.bfloat16
+U32 = mybir.dt.uint32
+U16 = mybir.dt.uint16
+U8 = mybir.dt.uint8
+FP8X4 = mybir.dt.float8_e4m3fn_x4
+ACT = mybir.ActivationFunctionType
+ALU = mybir.AluOpType
+AX = mybir.AxisListType
+
+P = 128
+PACK = 4
+BLOCKS = I // P
+CHUNKS = ((0, 1), (2,), (3,))
+PRODUCT_STEPS = (((0, 4),), ((0, 4),), ((0, 3), (3, 4)))
+
+
+def tile_attend_similarmerge_kernel(tc, query, keys, steep, th, dsc, offs, offs2, out):
+    nc = tc.nc
+    with ExitStack() as ctx:
+        sb = ctx.enter_context(tc.tile_pool(name="sb", bufs=1))
+        ps = ctx.enter_context(tc.psum_pool(name="ps", bufs=1))
+
+        def bank(tag, name, shape):
+            return ps.tile(shape, F32, name=name, tag=tag)
+
+        list_a = sb.tile([P, I // 16], U16, name="list_a")
+        list_b = sb.tile([P, I // 16], U16, name="list_b")
+        planes = [sb.tile([P, T], F32, name="plane%d" % t, tag="plane%d" % t, align_bytes=64) for t in range(PACK)]
+        got_a = sb.tile([P, PACK, 2 * P], F32, name="got_a", tag="got_a", align_bytes=64)
+        got_b = sb.tile([P, PACK, 2 * P], F32, name="got_b", tag="got_b", align_bytes=64)
+        dsc_col = sb.tile([P, PACK], F32, name="dsc_col")
+        rows = sb.tile([P, P], F32, name="rows")
+        q_raw = sb.tile([P, PACK, Q], F32, name="q_raw")
+        ident = sb.tile([P, P], F32, name="ident")
+
+        nc.gpsimd.memset(rows[:], 0.0)
+        make_identity(nc, ident[:])
+
+        keys_by_plane = keys.rearrange("(p t) n -> t p n", t=PACK)
+        nc.sync.dma_start(planes[0][:], keys_by_plane[0])
+        nc.sync.dma_start(list_a[:], offs)
+        nc.sync.dma_start(list_b[:], offs2)
+        nc.sync.dma_start(dsc_col[:], dsc.rearrange("o (p t) -> (o p) t", t=PACK))
+        nc.sync.dma_start(rows[0:BLOCKS, :], th.rearrange("(b p) o -> b (p o)", p=P))
+        nc.sync.dma_start(rows[BLOCKS : 2 * BLOCKS, :], steep.rearrange("(b p) o -> b (p o)", p=P))
+        for t in range(1, PACK):
+            nc.sync.dma_start(planes[t][:], keys_by_plane[t])
+        nc.sync.dma_start(q_raw[:], query.rearrange("(p t) q -> p t q", t=PACK))
+
+        warm_in = sb.tile([P, 1], F32, name="warm_in")
+        warm_out = sb.tile([P, 1], F32, name="warm_out")
+        nc.gpsimd.memset(warm_in[:], 0.0)
+        nc.scalar.activation(warm_out[:], warm_in[:], ACT.Exp)
+
+        neg_dsc = sb.tile([P, PACK], F32, name="neg_dsc")
+        nc.scalar.activation(neg_dsc[:], dsc_col[:], ACT.Copy, scale=-1.0)
+
+        step = [sb.tile([P, PACK + 1, P], F32, name="step%d" % b) for b in range(BLOCKS)]
+        nka = [sb.tile([P, PACK, 2 * P], F32, name="nka0"), sb.tile([P, PACK, P], F32, name="nka1"), step[1][:, 0:PACK, :]]
+        kbd0 = sb.tile([P, PACK, 2 * P], F32, name="kbd0")
+        kbd1 = sb.tile([P, PACK - 1, P], F32, name="kbd1")
+        kbd = [
+            [kbd0[:, t, :] for t in range(PACK)],
+            [kbd1[:, 0, :], kbd1[:, 1, :], kbd1[:, 2, :], step[0][:, 3, :]],
+            [step[0][:, 0, :], step[0][:, 1, :], step[0][:, 2, :], step[1][:, PACK, :]],
+        ]
+        spare = sb.tile([P, P + 8], F32, name="spare")
+        scratch = [
+            (nka[1][:, 1, :], spare[:, P : P + 1], spare[:, P + 1 : P + 2], nka[1][:, 2, 0:1]),
+            (kbd[1][1], spare[:, P + 2 : P + 3], kbd[1][2][:, 0:1], nka[1][:, 3, 0:1]),
+            (kbd[2][1], nka[2][:, 2, 0:1], kbd[2][2][:, 0:1], step[1][:, PACK - 1 : PACK + 1, 0]),
+            (spare[:, 0:P], spare[:, P + 3 : P + 4], spare[:, P + 4 : P + 5], spare[:, P + 5 : P + 6]),
+        ]
+        diff_bank = ("c", "e", "f", "c")
+        sum_bank = ("a", "b", "e", "f")
+        neg_ka = {}
+        sum_ps = {}
+        diff_ps = {}
+        back_ps = {}
+
+        def gather(c):
+            blocks = CHUNKS[c]
+            n = P * len(blocks)
+            cols = slice(blocks[0] * P // 16, (blocks[0] * P + n) // 16)
+            for j, b in enumerate(blocks):
+                neg_ka[b] = nka[c][:, :, j * P : (j + 1) * P]
+                diff_ps[b] = bank(diff_bank[b], "diff%d" % b, [P, PACK, P])
+                sum_ps[b] = bank(sum_bank[b], "sum%d" % b, [P, P])
+            place = slice(blocks[0] % 2 * P, blocks[0] % 2 * P + n)
+            ka = [got_a[:, t, place] for t in range(PACK)]
+            kb = [got_b[:, t, place] for t in range(PACK)]
+
+            def product(first, end):
+                for b in blocks:
+                    at = slice(b % 2 * P, (b % 2 + 1) * P)
+                    pr = sb.tile([P, end - first, P], F32, name="pr%d_%d" % (b, first), tag="pr%d_%d" % (b, first), align_bytes=64)
+                    nc.vector.tensor_tensor(pr[:], got_a[:, first:end, at], got_b[:, first:end, at], ALU.mult)
+                    for t in range(first, end):
+                        nc.tensor.matmul(sum_ps[b][:], pr[:, t - first, :], ident[:],
+                                         start=(t == 0), stop=(t == PACK - 1), is_transpose=True)
+
+            def difference(t):
+                for j, b in enumerate(blocks):
+                    nc.tensor.matmul(diff_ps[b][:, t, :], neg_ka[b][:, t, :], ident[:],
+                                     start=True, stop=False, is_transpose=True)
+                    nc.tensor.matmul(diff_ps[b][:, t, :], kbd[c][t][:, j * P : (j + 1) * P], ident[:],
+                                     start=False, stop=True, is_transpose=True)
+
+            for t in range(PACK):
+                nc.vector.tensor_copy(ka[t], planes[t][:].indirect(list_a[:, cols]))
+                nc.scalar.activation(nka[c][:, t, :], ka[t], ACT.Copy, scale=neg_dsc[:, t : t + 1])
+                for first, end in PRODUCT_STEPS[c]:
+                    if end == t:
+                        product(first, end)
+                if t > 0:
+                    difference(t - 1)
+                nc.vector.tensor_copy(kb[t], planes[t][:].indirect(list_b[:, cols]))
+                nc.scalar.activation(kbd[c][t], kb[t], ACT.Copy, scale=dsc_col[:, t : t + 1])
+            product(*PRODUCT_STEPS[c][-1])
+            difference(PACK - 1)
+
+        cols_ps = bank("x", "cols_ps", [P, P])
+        nc.tensor.transpose(cols_ps[:], rows[:], ident[:])
+        neg_th = sb.tile([P, BLOCKS], F32, name="neg_th")
+        half_steep = sb.tile([P, BLOCKS], F32, name="half_steep")
+
+        def slot_columns():
+            nc.scalar.activation(neg_th[:], cols_ps[:, 0:BLOCKS], ACT.Copy, scale=-1.0 / P)
+            nc.scalar.activation(half_steep[:], cols_ps[:, BLOCKS : 2 * BLOCKS], ACT.Copy, scale=0.5)
+
+        def share(b):
+            terms, gap, tanh, al = scratch[b]
+            nc.scalar.activation(terms, sum_ps[b][:], ACT.Identity, scale=1.0 / D,
+                                 bias=neg_th[:, b : b + 1], accum_out=gap)
+            nc.scalar.activation(tanh, gap, ACT.Tanh, scale=half_steep[:, b : b + 1])
+            copies = al.shape[1]
+            nc.scalar.activation(al, tanh.to_broadcast([P, copies]), ACT.Copy, scale=0.25, bias=0.25)
+            pieces = ((0, 1), (2, 3)) if b >= 2 else ((0, 1, 2, 3),)
+            back_ps[b] = bank(sum_bank[b], "back%d" % b, [P, PACK, P])
+            for n, piece in enumerate(pieces):
+                ts = slice(piece[0], piece[-1] + 1)
+                nc.scalar.activation(step[b][:, ts, :], diff_ps[b][:, ts, :], ACT.Copy, scale=al[:, n % copies : n % copies + 1])
+                for t in piece:
+                    nc.tensor.transpose(back_ps[b][:, t, :], step[b][:, t, :], ident[:])
+
+        q_grouped = sb.tile([P, Q, PACK], BF16, name="q_grouped", align_bytes=64)
+        q_codes = sb.tile([P, Q], U32, name="q_codes", tag="plane%d" % (PACK - 2), align_bytes=64)
+        q_scales = sb.tile([P, Q], U8, name="q_scales", align_bytes=64)
+
+        slot_columns()
+        gather(0)
+        for j in range(4):
+            qs = slice(j * Q // 4, (j + 1) * Q // 4)
+            nc.scalar.copy(q_grouped[:, qs, :].rearrange("p (c i) t -> p c t i", i=4),
+                           q_raw[:, :, qs].rearrange("p t (c i) -> p c t i", i=4))
+        share(0)
+        share(1)
+        gather(1)
+        share(2)
+        gather(2)
+        share(3)
+
+        km = sb.tile([P, I, PACK], BF16, name="km", tag="plane%d" % (PACK - 1), align_bytes=64)
+        k_codes = [sb.tile([P, len(bl) * P], U32, name="k_codes%d" % c, tag=("pr3_3", "pr3_0", "pr2_0")[c], align_bytes=64) for c, bl in enumerate(CHUNKS)]
+        k_scales = [sb.tile([P, len(bl) * P], U8, name="k_scales%d" % c, align_bytes=64) for c, bl in enumerate(CHUNKS)]
+        scores = [bank("x", "scores0", [P, I]), bank("y", "scores1", [P, I])]
+
+        def merge(c, j):
+            b = CHUNKS[c][j]
+            nc.vector.tensor_tensor(
+                km[:, b * P : (b + 1) * P, :].rearrange("p (c i) t -> p c t i", i=4),
+                back_ps[b][:].rearrange("p t (c i) -> p c t i", i=4),
+                neg_ka[b].rearrange("p t (c i) -> p c t i", i=4),
+                ALU.subtract,
+            )
+
+        def quantize(c):
+            nc.vector.quantize_mx(out=k_codes[c][:].bitcast(FP8X4), scales=k_scales[c][:],
+                                  in_=km[:, CHUNKS[c][0] * P : (CHUNKS[c][-1] + 1) * P, :].rearrange("p i t -> p (i t)"))
+
+        def score(c):
+            first = CHUNKS[c][0] * P
+            n = len(CHUNKS[c]) * P
+            for h in range(Q // P):
+                nc.tensor.matmul_mx(
+                    out=scores[h][:, first : first + n],
+                    lhsT=q_codes[:, h * P : (h + 1) * P].bitcast(FP8X4),
+                    lhsT_scale=q_scales[:, h * P : (h + 1) * P],
+                    rhs=k_codes[c][:].bitcast(FP8X4),
+                    rhs_scale=k_scales[c][:],
+                    start=True,
+                    stop=True,
+                )
+
+        nc.vector.quantize_mx(out=q_codes[:].bitcast(FP8X4), scales=q_scales[:],
+                              in_=q_grouped[:].rearrange("p q t -> p (q t)"))
+        merge(0, 0)
+        merge(0, 1)
+        merge(1, 0)
+        quantize(0)
+        score(0)
+        quantize(1)
+        score(1)
+        early = (BLOCKS - 1) * P
+        neg_early = [sb.tile([P, 1], F32, name="neg_early%d" % h) for h in range(Q // P)]
+        for h in range(Q // P):
+            nc.vector.tensor_reduce(neg_early[h][:], scores[h][:, 0:early], AX.X, ALU.max, negate=True)
+        merge(2, 0)
+        quantize(2)
+        score(2)
+
+        for h in range(Q // P):
+            neg_late = sb.tile([P, P], F32, name="neg_late%d" % h)
+            neg_max = sb.tile([P, 1], F32, name="neg_max%d" % h)
+            nc.vector.tensor_scalar(neg_late[:], scores[h][:, early:I], -1.0, neg_early[h][:],
+                                    ALU.mult, ALU.min, accum_out=neg_max[:])
+            p = sb.tile([P, I], F32, name="p%d" % h)
+            total = sb.tile([P, 1], F32, name="total%d" % h)
+            nc.scalar.activation(p[:], scores[h][:], ACT.Exp, bias=neg_max[:], accum_out=total[:])
+            inv = sb.tile([P, 1], F32, name="inv%d" % h)
+            nc.vector.reciprocal(inv[:], total[:])
+            y = sb.tile([P, I], F32, name="y%d" % h)
+            nc.vector.tensor_scalar(y[:], p[:], inv[:], float(I), ALU.mult, ALU.mult)
+            nc.sync.dma_start(out[h * P : (h + 1) * P, :], y[:])

@@ -42,7 +42,7 @@ def tile_attend_similarmerge_kernel(tc, query, keys, steep, th, dsc, offs, offs2
         q_raw = sb.tile([P, PACK, Q], F32, name="q_raw")
         ident = sb.tile([P, P], F32, name="ident")
 
-        nc.gpsimd.memset(rows[:], 0.0)
+        nc.vector.memset(rows[:], 0.0)
         make_identity(nc, ident[:])
 
         keys_by_plane = keys.rearrange("(p t) n -> t p n", t=PACK)
@@ -160,8 +160,8 @@ def tile_attend_similarmerge_kernel(tc, query, keys, steep, th, dsc, offs, offs2
         gather(0)
         for j in range(4):
             qs = slice(j * Q // 4, (j + 1) * Q // 4)
-            nc.scalar.copy(q_grouped[:, qs, :].rearrange("p (c i) t -> p c t i", i=4),
-                           q_raw[:, :, qs].rearrange("p t (c i) -> p c t i", i=4))
+            nc.scalar.copy(q_grouped[:, qs, :].rearrange("p (c i) t -> p c t i", i=2),
+                           q_raw[:, :, qs].rearrange("p t (c i) -> p c t i", i=2))
         share(0)
         share(1)
         gather(1)
@@ -177,9 +177,9 @@ def tile_attend_similarmerge_kernel(tc, query, keys, steep, th, dsc, offs, offs2
         def merge(c, j):
             b = CHUNKS[c][j]
             nc.vector.tensor_tensor(
-                km[:, b * P : (b + 1) * P, :].rearrange("p (c i) t -> p c t i", i=4),
-                back_ps[b][:].rearrange("p t (c i) -> p c t i", i=4),
-                neg_ka[b].rearrange("p t (c i) -> p c t i", i=4),
+                km[:, b * P : (b + 1) * P, :].rearrange("p (c i) t -> p c t i", i=2),
+                back_ps[b][:].rearrange("p t (c i) -> p c t i", i=2),
+                neg_ka[b].rearrange("p t (c i) -> p c t i", i=2),
                 ALU.subtract,
             )
 

@@ -20,13 +20,14 @@ P = 128
 PACK = 4
 BLOCKS = I // P
 CHUNKS = ((0, 1), (2,), (3,))
-PRODUCT_STEPS = (((0, 4),), ((0, 4),), ((0, 3), (3, 4)))
+PLANE_ORDER = ((0, 1, 2, 3), (3, 0, 1, 2))
 
 
 def tile_attend_similarmerge_kernel(tc, query, keys, steep, th, dsc, offs, offs2, out):
     nc = tc.nc
     with ExitStack() as ctx:
         sb = ctx.enter_context(tc.tile_pool(name="sb", bufs=1))
+        shared = ctx.enter_context(tc.tile_pool(name="shared", bufs=1))
         ps = ctx.enter_context(tc.psum_pool(name="ps", bufs=1))
 
         def bank(tag, name, shape):
@@ -34,9 +35,8 @@ def tile_attend_similarmerge_kernel(tc, query, keys, steep, th, dsc, offs, offs2
 
         list_a = sb.tile([P, I // 16], U16, name="list_a")
         list_b = sb.tile([P, I // 16], U16, name="list_b")
-        planes = [sb.tile([P, T], F32, name="plane%d" % t, tag="plane%d" % t, align_bytes=64) for t in range(PACK)]
-        got_a = sb.tile([P, PACK, 2 * P], F32, name="got_a", tag="got_a", align_bytes=64)
-        got_b = sb.tile([P, PACK, 2 * P], F32, name="got_b", tag="got_b", align_bytes=64)
+        planes = [sb.tile([P, T], F32, name="plane%d" % t, tag="plane%d" % t, align_bytes=64) for t in (0, 1, 3)]
+        planes = planes[:2] + [shared.tile([P, T], F32, name="plane2", align_bytes=64, offset=0)] + planes[2:]
         dsc_col = sb.tile([P, PACK], F32, name="dsc_col")
         rows = sb.tile([P, P], F32, name="rows")
         q_raw = sb.tile([P, PACK, Q], F32, name="q_raw")
@@ -64,71 +64,61 @@ def tile_attend_similarmerge_kernel(tc, query, keys, steep, th, dsc, offs, offs2
         neg_dsc = sb.tile([P, PACK], F32, name="neg_dsc")
         nc.scalar.activation(neg_dsc[:], dsc_col[:], ACT.Copy, scale=-1.0)
 
-        step = [sb.tile([P, PACK + 1, P], F32, name="step%d" % b) for b in range(BLOCKS)]
-        nka = [sb.tile([P, PACK, 2 * P], F32, name="nka0"), sb.tile([P, PACK, P], F32, name="nka1"), step[1][:, 0:PACK, :]]
-        kbd0 = sb.tile([P, PACK, 2 * P], F32, name="kbd0")
-        kbd1 = sb.tile([P, PACK - 1, P], F32, name="kbd1")
+        W = 2 * P
+        step = [sb.tile([P, PACK, P], F32, name="step%d" % b) for b in range(BLOCKS)]
+        nka = [sb.tile([P, PACK, W], F32, name="nka%d" % c, tag="nka%d" % c, align_bytes=64) for c in range(2)]
+        row = lambda name: sb.tile([P, W], F32, name=name, tag=name, align_bytes=64)
+        ka0 = [row("ka0_%d" % t) for t in range(PACK)]
+        kb0 = [row("kb0_%d" % t) for t in range(PACK)]
+        pr0 = [row("pr0_%d" % t) for t in range(PACK)]
+        kbd0 = [row("kbd0_%d" % t) for t in range(PACK)]
+        pr1 = [row("pr1_%d" % t) for t in range(PACK)]
+        ka1_first, kb1_first = row("ka1_first"), row("kb1_first")
+        ka = [ka0, [ka0[3], pr0[3], ka0[3], ka1_first]]
+        kb = [kb0, [kb0[3], kbd0[3], kb0[3], kb1_first]]
+        pr = [pr0, pr1]
         kbd = [
-            [kbd0[:, t, :] for t in range(PACK)],
-            [kbd1[:, 0, :], kbd1[:, 1, :], kbd1[:, 2, :], step[0][:, 3, :]],
-            [step[0][:, 0, :], step[0][:, 1, :], step[0][:, 2, :], step[1][:, PACK, :]],
+            [x[:] for x in kbd0],
+            [row("kbd1_0")[:], row("kbd1_1")[:], step[0][:, 0:2, :].rearrange("p t s -> p (t s)"), row("kbd1_3")[:]],
         ]
-        spare = sb.tile([P, P + 8], F32, name="spare")
+        spare = sb.tile([P, 2 * P + 16], F32, name="spare")
+        col = lambda j: spare[:, 2 * P + j : 2 * P + j + 1]
         scratch = [
-            (nka[1][:, 1, :], spare[:, P : P + 1], spare[:, P + 1 : P + 2], nka[1][:, 2, 0:1]),
-            (kbd[1][1], spare[:, P + 2 : P + 3], kbd[1][2][:, 0:1], nka[1][:, 3, 0:1]),
-            (kbd[2][1], nka[2][:, 2, 0:1], kbd[2][2][:, 0:1], step[1][:, PACK - 1 : PACK + 1, 0]),
-            (spare[:, 0:P], spare[:, P + 3 : P + 4], spare[:, P + 4 : P + 5], spare[:, P + 5 : P + 6]),
+            (nka[1][:, 0, 0:P], col(0), col(1), nka[1][:, 1, 0:1]),
+            (kbd[1][0][:, 0:P], col(2), kbd[1][1][:, 0:1], nka[1][:, 2, 0:1]),
+            (spare[:, 0:P], col(3), col(4), col(5)),
+            (spare[:, P : 2 * P], col(6), col(7), col(8)),
         ]
-        diff_bank = ("c", "e", "f", "c")
-        sum_bank = ("a", "b", "e", "f")
         neg_ka = {}
         sum_ps = {}
         diff_ps = {}
         back_ps = {}
 
         def gather(c):
-            blocks = CHUNKS[c]
-            n = P * len(blocks)
-            cols = slice(blocks[0] * P // 16, (blocks[0] * P + n) // 16)
+            blocks = (2 * c, 2 * c + 1)
+            order = PLANE_ORDER[c]
+            cols = slice(c * W // 16, (c + 1) * W // 16)
             for j, b in enumerate(blocks):
                 neg_ka[b] = nka[c][:, :, j * P : (j + 1) * P]
-                diff_ps[b] = bank(diff_bank[b], "diff%d" % b, [P, PACK, P])
-                sum_ps[b] = bank(sum_bank[b], "sum%d" % b, [P, P])
-            place = slice(blocks[0] % 2 * P, blocks[0] % 2 * P + n)
-            ka = [got_a[:, t, place] for t in range(PACK)]
-            kb = [got_b[:, t, place] for t in range(PACK)]
-
-            def product(first, end):
-                for b in blocks:
-                    at = slice(b % 2 * P, (b % 2 + 1) * P)
-                    pr = sb.tile([P, end - first, P], F32, name="pr%d_%d" % (b, first), tag="pr%d_%d" % (b, first), align_bytes=64)
-                    nc.vector.tensor_tensor(pr[:], got_a[:, first:end, at], got_b[:, first:end, at], ALU.mult)
-                    for t in range(first, end):
-                        nc.tensor.matmul(sum_ps[b][:], pr[:, t - first, :], ident[:],
-                                         start=(t == 0), stop=(t == PACK - 1), is_transpose=True)
-
-            def difference(t):
+                diff_ps[b] = bank("d%d" % b, "diff%d" % b, [P, PACK, P])
+                sum_ps[b] = bank("s%d" % b, "sum%d" % b, [P, P])
+            for t in order:
+                nc.vector.tensor_copy(ka[c][t][:], planes[t][:].indirect(list_a[:, cols]))
+                nc.scalar.activation(nka[c][:, t, :], ka[c][t][:], ACT.Copy, scale=neg_dsc[:, t : t + 1])
+                nc.vector.tensor_copy(kb[c][t][:], planes[t][:].indirect(list_b[:, cols]))
+                nc.scalar.activation(kbd[c][t], kb[c][t][:], ACT.Copy, scale=dsc_col[:, t : t + 1])
+                engine = nc.vector if (c == 1 and t == order[-1]) else nc.gpsimd
+                engine.tensor_tensor(pr[c][t][:], ka[c][t][:], kb[c][t][:], ALU.mult)
+                for j, b in enumerate(blocks):
+                    nc.tensor.matmul(sum_ps[b][:], pr[c][t][:, j * P : (j + 1) * P], ident[:],
+                                     start=(t == order[0]), stop=(t == order[-1]), is_transpose=True)
                 for j, b in enumerate(blocks):
                     nc.tensor.matmul(diff_ps[b][:, t, :], neg_ka[b][:, t, :], ident[:],
                                      start=True, stop=False, is_transpose=True)
                     nc.tensor.matmul(diff_ps[b][:, t, :], kbd[c][t][:, j * P : (j + 1) * P], ident[:],
                                      start=False, stop=True, is_transpose=True)
 
-            for t in range(PACK):
-                nc.vector.tensor_copy(ka[t], planes[t][:].indirect(list_a[:, cols]))
-                nc.scalar.activation(nka[c][:, t, :], ka[t], ACT.Copy, scale=neg_dsc[:, t : t + 1])
-                for first, end in PRODUCT_STEPS[c]:
-                    if end == t:
-                        product(first, end)
-                if t > 0:
-                    difference(t - 1)
-                nc.vector.tensor_copy(kb[t], planes[t][:].indirect(list_b[:, cols]))
-                nc.scalar.activation(kbd[c][t], kb[t], ACT.Copy, scale=dsc_col[:, t : t + 1])
-            product(*PRODUCT_STEPS[c][-1])
-            difference(PACK - 1)
-
-        cols_ps = bank("x", "cols_ps", [P, P])
+        cols_ps = bank("d2", "cols_ps", [P, P])
         nc.tensor.transpose(cols_ps[:], rows[:], ident[:])
         neg_th = sb.tile([P, BLOCKS], F32, name="neg_th")
         half_steep = sb.tile([P, BLOCKS], F32, name="half_steep")
@@ -142,18 +132,17 @@ def tile_attend_similarmerge_kernel(tc, query, keys, steep, th, dsc, offs, offs2
             nc.scalar.activation(terms, sum_ps[b][:], ACT.Identity, scale=1.0 / D,
                                  bias=neg_th[:, b : b + 1], accum_out=gap)
             nc.scalar.activation(tanh, gap, ACT.Tanh, scale=half_steep[:, b : b + 1])
-            copies = al.shape[1]
-            nc.scalar.activation(al, tanh.to_broadcast([P, copies]), ACT.Copy, scale=0.25, bias=0.25)
-            pieces = ((0, 1), (2, 3)) if b >= 2 else ((0, 1, 2, 3),)
-            back_ps[b] = bank(sum_bank[b], "back%d" % b, [P, PACK, P])
-            for n, piece in enumerate(pieces):
+            nc.scalar.activation(al, tanh, ACT.Copy, scale=0.25, bias=0.25)
+            pieces = ((0, 1), (2, 3)) if b == 3 else ((0, 1, 2, 3),)
+            back_ps[b] = bank("s%d" % b, "back%d" % b, [P, PACK, P])
+            for piece in pieces:
                 ts = slice(piece[0], piece[-1] + 1)
-                nc.scalar.activation(step[b][:, ts, :], diff_ps[b][:, ts, :], ACT.Copy, scale=al[:, n % copies : n % copies + 1])
+                nc.scalar.activation(step[b][:, ts, :], diff_ps[b][:, ts, :], ACT.Copy, scale=al)
                 for t in piece:
                     nc.tensor.transpose(back_ps[b][:, t, :], step[b][:, t, :], ident[:])
 
         q_grouped = sb.tile([P, Q, PACK], BF16, name="q_grouped", align_bytes=64)
-        q_codes = sb.tile([P, Q], U32, name="q_codes", tag="plane%d" % (PACK - 2), align_bytes=64)
+        q_codes = shared.tile([P, Q], U32, name="q_codes", align_bytes=64, offset=2048)
         q_scales = sb.tile([P, Q], U8, name="q_scales", align_bytes=64)
 
         slot_columns()
@@ -166,18 +155,17 @@ def tile_attend_similarmerge_kernel(tc, query, keys, steep, th, dsc, offs, offs2
         share(1)
         gather(1)
         share(2)
-        gather(2)
         share(3)
 
-        km = sb.tile([P, I, PACK], BF16, name="km", tag="plane%d" % (PACK - 1), align_bytes=64)
-        k_codes = [sb.tile([P, len(bl) * P], U32, name="k_codes%d" % c, tag=("pr3_3", "pr3_0", "pr2_0")[c], align_bytes=64) for c, bl in enumerate(CHUNKS)]
+        km = shared.tile([P, W, PACK], BF16, name="km", align_bytes=64, offset=0)
+        k_codes = [sb.tile([P, len(bl) * P], U32, name="k_codes%d" % c, tag=("pr1_2", "nka1", "pr1_1")[c], align_bytes=64) for c, bl in enumerate(CHUNKS)]
         k_scales = [sb.tile([P, len(bl) * P], U8, name="k_scales%d" % c, align_bytes=64) for c, bl in enumerate(CHUNKS)]
-        scores = [bank("x", "scores0", [P, I]), bank("y", "scores1", [P, I])]
+        scores = [bank("d0", "scores0", [P, I]), bank("d1", "scores1", [P, I])]
 
         def merge(c, j):
             b = CHUNKS[c][j]
             nc.vector.tensor_tensor(
-                km[:, b * P : (b + 1) * P, :].rearrange("p (c i) t -> p c t i", i=2),
+                km[:, b % 2 * P : (b % 2 + 1) * P, :].rearrange("p (c i) t -> p c t i", i=2),
                 back_ps[b][:].rearrange("p t (c i) -> p c t i", i=2),
                 neg_ka[b].rearrange("p t (c i) -> p c t i", i=2),
                 ALU.subtract,
@@ -185,7 +173,7 @@ def tile_attend_similarmerge_kernel(tc, query, keys, steep, th, dsc, offs, offs2
 
         def quantize(c):
             nc.vector.quantize_mx(out=k_codes[c][:].bitcast(FP8X4), scales=k_scales[c][:],
-                                  in_=km[:, CHUNKS[c][0] * P : (CHUNKS[c][-1] + 1) * P, :].rearrange("p i t -> p (i t)"))
+                                  in_=km[:, CHUNKS[c][0] % 2 * P : (CHUNKS[c][-1] % 2 + 1) * P, :].rearrange("p i t -> p (i t)"))
 
         def score(c):
             first = CHUNKS[c][0] * P
@@ -205,24 +193,18 @@ def tile_attend_similarmerge_kernel(tc, query, keys, steep, th, dsc, offs, offs2
                               in_=q_grouped[:].rearrange("p q t -> p (q t)"))
         merge(0, 0)
         merge(0, 1)
-        merge(1, 0)
         quantize(0)
         score(0)
+        merge(1, 0)
+        merge(2, 0)
         quantize(1)
         score(1)
-        early = (BLOCKS - 1) * P
-        neg_early = [sb.tile([P, 1], F32, name="neg_early%d" % h) for h in range(Q // P)]
-        for h in range(Q // P):
-            nc.vector.tensor_reduce(neg_early[h][:], scores[h][:, 0:early], AX.X, ALU.max, negate=True)
-        merge(2, 0)
         quantize(2)
         score(2)
 
         for h in range(Q // P):
-            neg_late = sb.tile([P, P], F32, name="neg_late%d" % h)
             neg_max = sb.tile([P, 1], F32, name="neg_max%d" % h)
-            nc.vector.tensor_scalar(neg_late[:], scores[h][:, early:I], -1.0, neg_early[h][:],
-                                    ALU.mult, ALU.min, accum_out=neg_max[:])
+            nc.vector.tensor_reduce(neg_max[:], scores[h][:], AX.X, ALU.max, negate=True)
             p = sb.tile([P, I], F32, name="p%d" % h)
             total = sb.tile([P, 1], F32, name="total%d" % h)
             nc.scalar.activation(p[:], scores[h][:], ACT.Exp, bias=neg_max[:], accum_out=total[:])

@@ -4,6 +4,7 @@ import concourse.mybir as mybir
 from concourse.masks import make_identity
 
 D, T, I, Q = 512, 1024, 512, 256
+OUT_SCALE = 512.0
 FLOPS = 2 * D * I * Q
 
 F32 = mybir.dt.float32
@@ -19,8 +20,13 @@ AX = mybir.AxisListType
 P = 128
 PACK = 4
 BLOCKS = I // P
-CHUNKS = ((0, 1), (2,), (3,))
+CHUNK = 2 * P
+HALVES = Q // P
+LIST_ROWS = 16
 PLANE_ORDER = ((0, 1, 2, 3), (3, 0, 1, 2))
+LAST_PLANE = PLANE_ORDER[1][-1]
+SCORE_GROUPS = ((0, 1), (2,), (3,))
+PAIR = 2
 
 
 def tile_attend_similarmerge_kernel(tc, query, keys, steep, th, dsc, offs, offs2, out):
@@ -33,16 +39,22 @@ def tile_attend_similarmerge_kernel(tc, query, keys, steep, th, dsc, offs, offs2
         def bank(tag, name, shape):
             return ps.tile(shape, F32, name=name, tag=tag)
 
-        list_a = sb.tile([P, I // 16], U16, name="list_a")
-        list_b = sb.tile([P, I // 16], U16, name="list_b")
-        planes = [sb.tile([P, T], F32, name="plane%d" % t, tag="plane%d" % t, align_bytes=64) for t in (0, 1, 3)]
-        planes = planes[:2] + [shared.tile([P, T], F32, name="plane2", align_bytes=64, offset=0)] + planes[2:]
+        def chunk_row(name):
+            return sb.tile([P, CHUNK], F32, name=name, tag=name, align_bytes=64)
+
+        list_a = sb.tile([P, I // LIST_ROWS], U16, name="list_a")
+        list_b = sb.tile([P, I // LIST_ROWS], U16, name="list_b")
+        planes = [
+            shared.tile([P, T], F32, name="last_plane", align_bytes=64, offset=0) if t == LAST_PLANE
+            else sb.tile([P, T], F32, name="plane%d" % t, align_bytes=64)
+            for t in range(PACK)
+        ]
         dsc_col = sb.tile([P, PACK], F32, name="dsc_col")
-        rows = sb.tile([P, P], F32, name="rows")
+        slot_rows = sb.tile([P, P], F32, name="slot_rows")
         q_raw = sb.tile([P, PACK, Q], F32, name="q_raw")
         ident = sb.tile([P, P], F32, name="ident")
 
-        nc.vector.memset(rows[:], 0.0)
+        nc.vector.memset(slot_rows[:], 0.0)
         make_identity(nc, ident[:])
 
         keys_by_plane = keys.rearrange("(p t) n -> t p n", t=PACK)
@@ -50,82 +62,73 @@ def tile_attend_similarmerge_kernel(tc, query, keys, steep, th, dsc, offs, offs2
         nc.sync.dma_start(list_a[:], offs)
         nc.sync.dma_start(list_b[:], offs2)
         nc.sync.dma_start(dsc_col[:], dsc.rearrange("o (p t) -> (o p) t", t=PACK))
-        nc.sync.dma_start(rows[0:BLOCKS, :], th.rearrange("(b p) o -> b (p o)", p=P))
-        nc.sync.dma_start(rows[BLOCKS : 2 * BLOCKS, :], steep.rearrange("(b p) o -> b (p o)", p=P))
+        nc.sync.dma_start(slot_rows[0:BLOCKS, :], th.rearrange("(b p) o -> b (p o)", p=P))
+        nc.sync.dma_start(slot_rows[BLOCKS : 2 * BLOCKS, :], steep.rearrange("(b p) o -> b (p o)", p=P))
         for t in range(1, PACK):
             nc.sync.dma_start(planes[t][:], keys_by_plane[t])
         nc.sync.dma_start(q_raw[:], query.rearrange("(p t) q -> p t q", t=PACK))
 
-        warm_in = sb.tile([P, 1], F32, name="warm_in")
-        warm_out = sb.tile([P, 1], F32, name="warm_out")
-        nc.gpsimd.memset(warm_in[:], 0.0)
-        nc.scalar.activation(warm_out[:], warm_in[:], ACT.Exp)
-
         neg_dsc = sb.tile([P, PACK], F32, name="neg_dsc")
         nc.scalar.activation(neg_dsc[:], dsc_col[:], ACT.Copy, scale=-1.0)
 
-        W = 2 * P
-        step = [sb.tile([P, PACK, P], F32, name="step%d" % b) for b in range(BLOCKS)]
-        nka = [sb.tile([P, PACK, W], F32, name="nka%d" % c, tag="nka%d" % c, align_bytes=64) for c in range(2)]
-        row = lambda name: sb.tile([P, W], F32, name=name, tag=name, align_bytes=64)
-        ka0 = [row("ka0_%d" % t) for t in range(PACK)]
-        kb0 = [row("kb0_%d" % t) for t in range(PACK)]
-        pr0 = [row("pr0_%d" % t) for t in range(PACK)]
-        kbd0 = [row("kbd0_%d" % t) for t in range(PACK)]
-        pr1 = [row("pr1_%d" % t) for t in range(PACK)]
-        ka1_first, kb1_first = row("ka1_first"), row("kb1_first")
-        ka = [ka0, [ka0[3], pr0[3], ka0[3], ka1_first]]
-        kb = [kb0, [kb0[3], kbd0[3], kb0[3], kb1_first]]
-        pr = [pr0, pr1]
+        move = [sb.tile([P, PACK, P], F32, name="move%d" % b, tag="move%d" % b, align_bytes=64) for b in range(BLOCKS)]
+        neg_kad = [sb.tile([P, PACK, CHUNK], F32, name="neg_kad%d" % c, tag="neg_kad%d" % c, align_bytes=64)
+                   for c in range(2)]
+        ka0 = [chunk_row("ka0_%d" % t) for t in range(PACK)]
+        kb0 = [chunk_row("kb0_%d" % t) for t in range(PACK)]
+        prod0 = [chunk_row("prod0_%d" % t) for t in range(PACK)]
+        kbd0 = [chunk_row("kbd0_%d" % t) for t in range(PACK)]
+        prod1 = [chunk_row("prod1_%d" % t) for t in range(PACK)]
+        ka = [ka0, [ka0[3], prod0[3], ka0[3], chunk_row("ka1_3")]]
+        kb = [kb0, [kb0[3], kbd0[3], kb0[3], chunk_row("kb1_3")]]
+        prod = [prod0, prod1]
         kbd = [
-            [x[:] for x in kbd0],
-            [row("kbd1_0")[:], row("kbd1_1")[:], step[0][:, 0:2, :].rearrange("p t s -> p (t s)"), row("kbd1_3")[:]],
+            [row[:] for row in kbd0],
+            [chunk_row("kbd1_0")[:], chunk_row("kbd1_1")[:],
+             move[0][:, 0:2, :].rearrange("p t s -> p (t s)"), chunk_row("kbd1_3")[:]],
         ]
-        spare = sb.tile([P, 2 * P + 16], F32, name="spare")
-        col = lambda j: spare[:, 2 * P + j : 2 * P + j + 1]
+        singles = 9
+        spare = sb.tile([P, 2 * P + singles], F32, name="spare")
+        single = [spare[:, 2 * P + j : 2 * P + j + 1] for j in range(singles)]
         scratch = [
-            (nka[1][:, 0, 0:P], col(0), col(1), nka[1][:, 1, 0:1]),
-            (kbd[1][0][:, 0:P], col(2), kbd[1][1][:, 0:1], nka[1][:, 2, 0:1]),
-            (spare[:, 0:P], col(3), col(4), col(5)),
-            (spare[:, P : 2 * P], col(6), col(7), col(8)),
+            (neg_kad[1][:, 0, 0:P], single[0], single[1], neg_kad[1][:, 1, 0:1]),
+            (kbd[1][0][:, 0:P], single[2], kbd[1][1][:, 0:1], neg_kad[1][:, 2, 0:1]),
+            (spare[:, 0:P], single[3], single[4], single[5]),
+            (spare[:, P : 2 * P], single[6], single[7], single[8]),
         ]
-        neg_ka = {}
-        sum_ps = {}
-        diff_ps = {}
-        back_ps = {}
+        sum_ps = []
+        diff_ps = []
+        move_ps = []
+
+        def add_transposed(target, source, start, stop):
+            nc.tensor.matmul(target, source, ident[:], start=start, stop=stop, is_transpose=True)
 
         def gather(c):
-            blocks = (2 * c, 2 * c + 1)
             order = PLANE_ORDER[c]
-            cols = slice(c * W // 16, (c + 1) * W // 16)
-            for j, b in enumerate(blocks):
-                neg_ka[b] = nka[c][:, :, j * P : (j + 1) * P]
-                diff_ps[b] = bank("d%d" % b, "diff%d" % b, [P, PACK, P])
-                sum_ps[b] = bank("s%d" % b, "sum%d" % b, [P, P])
+            blocks = (2 * c, 2 * c + 1)
+            entries = slice(c * CHUNK // LIST_ROWS, (c + 1) * CHUNK // LIST_ROWS)
+            for b in blocks:
+                diff_ps.append(bank("d%d" % b, "diff%d" % b, [P, PACK, P]))
+                sum_ps.append(bank("s%d" % b, "sum%d" % b, [P, P]))
             for t in order:
-                nc.vector.tensor_copy(ka[c][t][:], planes[t][:].indirect(list_a[:, cols]))
-                nc.scalar.activation(nka[c][:, t, :], ka[c][t][:], ACT.Copy, scale=neg_dsc[:, t : t + 1])
-                nc.vector.tensor_copy(kb[c][t][:], planes[t][:].indirect(list_b[:, cols]))
+                nc.vector.tensor_copy(ka[c][t][:], planes[t][:].indirect(list_a[:, entries]))
+                nc.scalar.activation(neg_kad[c][:, t, :], ka[c][t][:], ACT.Copy, scale=neg_dsc[:, t : t + 1])
+                nc.vector.tensor_copy(kb[c][t][:], planes[t][:].indirect(list_b[:, entries]))
                 nc.scalar.activation(kbd[c][t], kb[c][t][:], ACT.Copy, scale=dsc_col[:, t : t + 1])
-                engine = nc.vector if (c == 1 and t == order[-1]) else nc.gpsimd
-                engine.tensor_tensor(pr[c][t][:], ka[c][t][:], kb[c][t][:], ALU.mult)
+                engine = nc.vector if (c, t) == (1, LAST_PLANE) else nc.gpsimd
+                engine.tensor_tensor(prod[c][t][:], ka[c][t][:], kb[c][t][:], ALU.mult)
                 for j, b in enumerate(blocks):
-                    nc.tensor.matmul(sum_ps[b][:], pr[c][t][:, j * P : (j + 1) * P], ident[:],
-                                     start=(t == order[0]), stop=(t == order[-1]), is_transpose=True)
+                    add_transposed(sum_ps[b][:], prod[c][t][:, j * P : (j + 1) * P], t == order[0], t == order[-1])
                 for j, b in enumerate(blocks):
-                    nc.tensor.matmul(diff_ps[b][:, t, :], neg_ka[b][:, t, :], ident[:],
-                                     start=True, stop=False, is_transpose=True)
-                    nc.tensor.matmul(diff_ps[b][:, t, :], kbd[c][t][:, j * P : (j + 1) * P], ident[:],
-                                     start=False, stop=True, is_transpose=True)
+                    add_transposed(diff_ps[b][:, t, :], neg_kad[c][:, t, j * P : (j + 1) * P], True, False)
+                    add_transposed(diff_ps[b][:, t, :], kbd[c][t][:, j * P : (j + 1) * P], False, True)
 
-        cols_ps = bank("d2", "cols_ps", [P, P])
-        nc.tensor.transpose(cols_ps[:], rows[:], ident[:])
         neg_th = sb.tile([P, BLOCKS], F32, name="neg_th")
         half_steep = sb.tile([P, BLOCKS], F32, name="half_steep")
-
-        def slot_columns():
-            nc.scalar.activation(neg_th[:], cols_ps[:, 0:BLOCKS], ACT.Copy, scale=-1.0 / P)
-            nc.scalar.activation(half_steep[:], cols_ps[:, BLOCKS : 2 * BLOCKS], ACT.Copy, scale=0.5)
+        slot_cols = bank("d2", "slot_cols", [P, P])
+        nc.tensor.transpose(slot_cols[:], slot_rows[:], ident[:])
+        nc.scalar.activation(neg_th[:], slot_cols[:, 0:BLOCKS], ACT.Copy, scale=-1.0 / P)
+        nc.scalar.activation(half_steep[:], slot_cols[:, BLOCKS : 2 * BLOCKS], ACT.Copy, scale=0.5)
 
         def share(b):
             terms, gap, tanh, al = scratch[b]
@@ -133,83 +136,94 @@ def tile_attend_similarmerge_kernel(tc, query, keys, steep, th, dsc, offs, offs2
                                  bias=neg_th[:, b : b + 1], accum_out=gap)
             nc.scalar.activation(tanh, gap, ACT.Tanh, scale=half_steep[:, b : b + 1])
             nc.scalar.activation(al, tanh, ACT.Copy, scale=0.25, bias=0.25)
-            pieces = ((0, 1), (2, 3)) if b == 3 else ((0, 1, 2, 3),)
-            back_ps[b] = bank("s%d" % b, "back%d" % b, [P, PACK, P])
-            for piece in pieces:
-                ts = slice(piece[0], piece[-1] + 1)
-                nc.scalar.activation(step[b][:, ts, :], diff_ps[b][:, ts, :], ACT.Copy, scale=al)
-                for t in piece:
-                    nc.tensor.transpose(back_ps[b][:, t, :], step[b][:, t, :], ident[:])
+            move_ps.append(bank("s%d" % b, "move_ps%d" % b, [P, PACK, P]))
+            width = 2 if b == BLOCKS - 1 else PACK
+            for first in range(0, PACK, width):
+                ts = slice(first, first + width)
+                nc.scalar.activation(move[b][:, ts, :], diff_ps[b][:, ts, :], ACT.Copy, scale=al)
+                for t in range(first, first + width):
+                    nc.tensor.transpose(move_ps[b][:, t, :], move[b][:, t, :], ident[:])
 
-        q_grouped = sb.tile([P, Q, PACK], BF16, name="q_grouped", align_bytes=64)
-        q_codes = shared.tile([P, Q], U32, name="q_codes", align_bytes=64, offset=2048)
-        q_scales = sb.tile([P, Q], U8, name="q_scales", align_bytes=64)
-
-        slot_columns()
         gather(0)
-        for j in range(4):
-            qs = slice(j * Q // 4, (j + 1) * Q // 4)
-            nc.scalar.copy(q_grouped[:, qs, :].rearrange("p (c i) t -> p c t i", i=2),
-                           q_raw[:, :, qs].rearrange("p t (c i) -> p c t i", i=2))
         share(0)
         share(1)
         gather(1)
         share(2)
         share(3)
 
-        km = shared.tile([P, W, PACK], BF16, name="km", align_bytes=64, offset=0)
-        k_codes = [sb.tile([P, len(bl) * P], U32, name="k_codes%d" % c, tag=("pr1_2", "nka1", "pr1_1")[c], align_bytes=64) for c, bl in enumerate(CHUNKS)]
-        k_scales = [sb.tile([P, len(bl) * P], U8, name="k_scales%d" % c, align_bytes=64) for c, bl in enumerate(CHUNKS)]
-        scores = [bank("d0", "scores0", [P, I]), bank("d1", "scores1", [P, I])]
+        km = shared.tile([P, CHUNK, PACK], BF16, name="km", align_bytes=64, offset=0)
+        q_grouped = shared.tile([P, Q, PACK], BF16, name="q_grouped", align_bytes=64, offset=2 * CHUNK * PACK)
+        q_codes = [sb.tile([P, P], U32, name="q_codes%d" % h, tag=tag, align_bytes=64)
+                   for h, tag in enumerate(("q_codes0", "move3"))]
+        q_scales = [sb.tile([P, P], U8, name="q_scales%d" % h, align_bytes=64) for h in range(HALVES)]
+        k_codes = [sb.tile([P, len(SCORE_GROUPS[g]) * P], U32, name="k_codes%d" % g, tag=tag, align_bytes=64)
+                   for g, tag in enumerate(("prod1_%d" % LAST_PLANE, "neg_kad1", "prod1_1"))]
+        k_scales = [sb.tile([P, len(blocks) * P], U8, name="k_scales%d" % g, align_bytes=64)
+                    for g, blocks in enumerate(SCORE_GROUPS)]
+        scores = [bank("d3", "scores0", [P, I]), bank("d1", "scores1", [P, I])]
 
-        def merge(c, j):
-            b = CHUNKS[c][j]
-            nc.vector.tensor_tensor(
-                km[:, b % 2 * P : (b % 2 + 1) * P, :].rearrange("p (c i) t -> p c t i", i=2),
-                back_ps[b][:].rearrange("p t (c i) -> p c t i", i=2),
-                neg_ka[b].rearrange("p t (c i) -> p c t i", i=2),
-                ALU.subtract,
+        def by_pairs_out(words):
+            return words.rearrange("p (c i) t -> p c t i", i=PAIR)
+
+        def by_pairs_in(rows):
+            return rows.rearrange("p t (c i) -> p c t i", i=PAIR)
+
+        def merge(b):
+            at = slice(b % 2 * P, (b % 2 + 1) * P)
+            nc.vector.tensor_tensor(by_pairs_out(km[:, at, :]), by_pairs_in(move_ps[b][:]),
+                                    by_pairs_in(neg_kad[b // 2][:, :, at]), ALU.subtract)
+
+        def quantize_query(h):
+            nc.vector.quantize_mx(out=q_codes[h][:].bitcast(FP8X4), scales=q_scales[h][:],
+                                  in_=q_grouped[:, h * P : (h + 1) * P, :].rearrange("p q t -> p (q t)"))
+
+        def quantize_keys(g):
+            blocks = SCORE_GROUPS[g]
+            at = slice(blocks[0] % 2 * P, (blocks[-1] % 2 + 1) * P)
+            nc.vector.quantize_mx(out=k_codes[g][:].bitcast(FP8X4), scales=k_scales[g][:],
+                                  in_=km[:, at, :].rearrange("p i t -> p (i t)"))
+
+        def score(g, h):
+            blocks = SCORE_GROUPS[g]
+            nc.tensor.matmul_mx(
+                out=scores[h][:, blocks[0] * P : (blocks[-1] + 1) * P],
+                lhsT=q_codes[h][:].bitcast(FP8X4),
+                lhsT_scale=q_scales[h][:],
+                rhs=k_codes[g][:].bitcast(FP8X4),
+                rhs_scale=k_scales[g][:],
+                start=True,
+                stop=True,
             )
 
-        def quantize(c):
-            nc.vector.quantize_mx(out=k_codes[c][:].bitcast(FP8X4), scales=k_scales[c][:],
-                                  in_=km[:, CHUNKS[c][0] % 2 * P : (CHUNKS[c][-1] % 2 + 1) * P, :].rearrange("p i t -> p (i t)"))
+        for h in range(HALVES):
+            rows_h = slice(h * P, (h + 1) * P)
+            nc.vector.tensor_copy(by_pairs_out(q_grouped[:, rows_h, :]), by_pairs_in(q_raw[:, :, rows_h]))
+        merge(0)
+        merge(1)
+        quantize_query(0)
+        quantize_keys(0)
+        score(0, 0)
+        merge(2)
+        merge(3)
+        quantize_query(1)
+        score(0, 1)
+        quantize_keys(1)
+        quantize_keys(2)
+        for h in range(HALVES):
+            score(1, h)
+            score(2, h)
 
-        def score(c):
-            first = CHUNKS[c][0] * P
-            n = len(CHUNKS[c]) * P
-            for h in range(Q // P):
-                nc.tensor.matmul_mx(
-                    out=scores[h][:, first : first + n],
-                    lhsT=q_codes[:, h * P : (h + 1) * P].bitcast(FP8X4),
-                    lhsT_scale=q_scales[:, h * P : (h + 1) * P],
-                    rhs=k_codes[c][:].bitcast(FP8X4),
-                    rhs_scale=k_scales[c][:],
-                    start=True,
-                    stop=True,
-                )
-
-        nc.vector.quantize_mx(out=q_codes[:].bitcast(FP8X4), scales=q_scales[:],
-                              in_=q_grouped[:].rearrange("p q t -> p (q t)"))
-        merge(0, 0)
-        merge(0, 1)
-        quantize(0)
-        score(0)
-        merge(1, 0)
-        merge(2, 0)
-        quantize(1)
-        score(1)
-        quantize(2)
-        score(2)
-
-        for h in range(Q // P):
+        for h in range(HALVES):
             neg_max = sb.tile([P, 1], F32, name="neg_max%d" % h)
             nc.vector.tensor_reduce(neg_max[:], scores[h][:], AX.X, ALU.max, negate=True)
-            p = sb.tile([P, I], F32, name="p%d" % h)
+            weights = sb.tile([P, I], F32, name="weights%d" % h)
             total = sb.tile([P, 1], F32, name="total%d" % h)
-            nc.scalar.activation(p[:], scores[h][:], ACT.Exp, bias=neg_max[:], accum_out=total[:])
-            inv = sb.tile([P, 1], F32, name="inv%d" % h)
-            nc.vector.reciprocal(inv[:], total[:])
-            y = sb.tile([P, I], F32, name="y%d" % h)
-            nc.vector.tensor_scalar(y[:], p[:], inv[:], float(I), ALU.mult, ALU.mult)
-            nc.sync.dma_start(out[h * P : (h + 1) * P, :], y[:])
+            nc.scalar.activation(weights[:], scores[h][:], ACT.Exp, bias=neg_max[:], accum_out=total[:])
+            inverse = sb.tile([P, 1], F32, name="inverse%d" % h)
+            nc.vector.reciprocal(inverse[:], total[:])
+            result = sb.tile([P, I], F32, name="result%d" % h)
+            width = I // 2 if h == HALVES - 1 else I
+            for first in range(0, I, width):
+                at = slice(first, first + width)
+                nc.vector.tensor_scalar(result[:, at], weights[:, at], inverse[:], OUT_SCALE, ALU.mult, ALU.mult)
+                nc.sync.dma_start(out[h * P : (h + 1) * P, at], result[:, at])

@@ -61,9 +61,9 @@ def tile_attend_similarmerge_kernel(tc, query, keys, steep, th, dsc, offs, offs2
         nc.sync.dma_start(planes[0][:], keys_by_plane[0])
         nc.sync.dma_start(list_a[:], offs)
         nc.sync.dma_start(list_b[:], offs2)
-        nc.sync.dma_start(dsc_col[:], dsc.rearrange("o (p t) -> (o p) t", t=PACK))
-        nc.sync.dma_start(slot_rows[0:BLOCKS, :], th.rearrange("(b p) o -> b (p o)", p=P))
-        nc.sync.dma_start(slot_rows[BLOCKS : 2 * BLOCKS, :], steep.rearrange("(b p) o -> b (p o)", p=P))
+        nc.scalar.dma_start(dsc_col[:], dsc.rearrange("o (p t) -> (o p) t", t=PACK))
+        nc.scalar.dma_start(slot_rows[0:BLOCKS, :], th.rearrange("(b p) o -> b (p o)", p=P))
+        nc.scalar.dma_start(slot_rows[BLOCKS : 2 * BLOCKS, :], steep.rearrange("(b p) o -> b (p o)", p=P))
         for t in range(1, PACK):
             nc.sync.dma_start(planes[t][:], keys_by_plane[t])
         nc.sync.dma_start(q_raw[:], query.rearrange("(p t) q -> p t q", t=PACK))

from contextlib import ExitStack

import concourse.mybir as mybir
from concourse.masks import make_identity

D, T, I, Q = 512, 1024, 512, 256
OUT_SCALE = 512.0
FLOPS = 2 * D * I * Q

F32 = mybir.dt.float32
BF16 = mybir.dt.bfloat16
U32 = mybir.dt.uint32
U16 = mybir.dt.uint16
U8 = mybir.dt.uint8
FP8X4 = mybir.dt.float8_e4m3fn_x4
ACT = mybir.ActivationFunctionType
ALU = mybir.AluOpType
AX = mybir.AxisListType

P = 128
PACK = 4
BLOCKS = I // P
CHUNK = 2 * P
HALVES = Q // P
LIST_ROWS = 16
PLANE_ORDER = ((0, 1, 2, 3), (3, 0, 1, 2))
LAST_PLANE = PLANE_ORDER[1][-1]
SCORE_GROUPS = ((0, 1), (2,), (3,))
PAIR = 2


def tile_attend_similarmerge_kernel(tc, query, keys, steep, th, dsc, offs, offs2, out):
    nc = tc.nc
    with ExitStack() as ctx:
        sb = ctx.enter_context(tc.tile_pool(name="sb", bufs=1))
        shared = ctx.enter_context(tc.tile_pool(name="shared", bufs=1))
        ps = ctx.enter_context(tc.psum_pool(name="ps", bufs=1))

        def bank(tag, name, shape):
            return ps.tile(shape, F32, name=name, tag=tag)

        def chunk_row(name):
            return sb.tile([P, CHUNK], F32, name=name, tag=name, align_bytes=64)

        list_a = sb.tile([P, I // LIST_ROWS], U16, name="list_a")
        list_b = sb.tile([P, I // LIST_ROWS], U16, name="list_b")
        planes = [
            shared.tile([P, T], F32, name="last_plane", align_bytes=64, offset=0) if t == LAST_PLANE
            else sb.tile([P, T], F32, name="plane%d" % t, align_bytes=64)
            for t in range(PACK)
        ]
        dsc_col = sb.tile([P, PACK], F32, name="dsc_col")
        slot_rows = sb.tile([P, P], F32, name="slot_rows")
        q_raw = sb.tile([P, PACK, Q], F32, name="q_raw")
        ident = sb.tile([P, P], F32, name="ident")

        nc.vector.memset(slot_rows[:], 0.0)
        make_identity(nc, ident[:])

        keys_by_plane = keys.rearrange("(p t) n -> t p n", t=PACK)
        nc.sync.dma_start(planes[0][:], keys_by_plane[0])
        nc.sync.dma_start(list_a[:], offs)
        nc.sync.dma_start(list_b[:], offs2)
        nc.scalar.dma_start(dsc_col[:], dsc.rearrange("o (p t) -> (o p) t", t=PACK))
        nc.scalar.dma_start(slot_rows[0:BLOCKS, :], th.rearrange("(b p) o -> b (p o)", p=P))
        nc.scalar.dma_start(slot_rows[BLOCKS : 2 * BLOCKS, :], steep.rearrange("(b p) o -> b (p o)", p=P))
        for t in range(1, PACK):
            nc.sync.dma_start(planes[t][:], keys_by_plane[t])
        nc.sync.dma_start(q_raw[:], query.rearrange("(p t) q -> p t q", t=PACK))

        neg_dsc = sb.tile([P, PACK], F32, name="neg_dsc")
        nc.scalar.activation(neg_dsc[:], dsc_col[:], ACT.Copy, scale=-1.0)

        move = [sb.tile([P, PACK, P], F32, name="move%d" % b, tag="move%d" % b, align_bytes=64) for b in range(BLOCKS)]
        neg_kad = [sb.tile([P, PACK, CHUNK], F32, name="neg_kad%d" % c, tag="neg_kad%d" % c, align_bytes=64)
                   for c in range(2)]
        ka0 = [chunk_row("ka0_%d" % t) for t in range(PACK)]
        kb0 = [chunk_row("kb0_%d" % t) for t in range(PACK)]
        prod0 = [chunk_row("prod0_%d" % t) for t in range(PACK)]
        kbd0 = [chunk_row("kbd0_%d" % t) for t in range(PACK)]
        prod1 = [chunk_row("prod1_%d" % t) for t in range(PACK)]
        ka = [ka0, [ka0[3], prod0[3], ka0[3], chunk_row("ka1_3")]]
        kb = [kb0, [kb0[3], kbd0[3], kb0[3], chunk_row("kb1_3")]]
        prod = [prod0, prod1]
        kbd = [
            [row[:] for row in kbd0],
            [chunk_row("kbd1_0")[:], chunk_row("kbd1_1")[:],
             move[0][:, 0:2, :].rearrange("p t s -> p (t s)"), chunk_row("kbd1_3")[:]],
        ]
        singles = 9
        spare = sb.tile([P, 2 * P + singles], F32, name="spare")
        single = [spare[:, 2 * P + j : 2 * P + j + 1] for j in range(singles)]
        scratch = [
            (neg_kad[1][:, 0, 0:P], single[0], single[1], neg_kad[1][:, 1, 0:1]),
            (kbd[1][0][:, 0:P], single[2], kbd[1][1][:, 0:1], neg_kad[1][:, 2, 0:1]),
            (spare[:, 0:P], single[3], single[4], single[5]),
            (spare[:, P : 2 * P], single[6], single[7], single[8]),
        ]
        sum_ps = []
        diff_ps = []
        move_ps = []

        def add_transposed(target, source, start, stop):
            nc.tensor.matmul(target, source, ident[:], start=start, stop=stop, is_transpose=True)

        def gather(c):
            order = PLANE_ORDER[c]
            blocks = (2 * c, 2 * c + 1)
            entries = slice(c * CHUNK // LIST_ROWS, (c + 1) * CHUNK // LIST_ROWS)
            for b in blocks:
                diff_ps.append(bank("d%d" % b, "diff%d" % b, [P, PACK, P]))
                sum_ps.append(bank("s%d" % b, "sum%d" % b, [P, P]))
            for t in order:
                nc.vector.tensor_copy(ka[c][t][:], planes[t][:].indirect(list_a[:, entries]))
                nc.scalar.activation(neg_kad[c][:, t, :], ka[c][t][:], ACT.Copy, scale=neg_dsc[:, t : t + 1])
                nc.vector.tensor_copy(kb[c][t][:], planes[t][:].indirect(list_b[:, entries]))
                nc.scalar.activation(kbd[c][t], kb[c][t][:], ACT.Copy, scale=dsc_col[:, t : t + 1])
                engine = nc.vector if (c, t) == (1, LAST_PLANE) else nc.gpsimd
                engine.tensor_tensor(prod[c][t][:], ka[c][t][:], kb[c][t][:], ALU.mult)
                for j, b in enumerate(blocks):
                    add_transposed(sum_ps[b][:], prod[c][t][:, j * P : (j + 1) * P], t == order[0], t == order[-1])
                for j, b in enumerate(blocks):
                    add_transposed(diff_ps[b][:, t, :], neg_kad[c][:, t, j * P : (j + 1) * P], True, False)
                    add_transposed(diff_ps[b][:, t, :], kbd[c][t][:, j * P : (j + 1) * P], False, True)

        neg_th = sb.tile([P, BLOCKS], F32, name="neg_th")
        half_steep = sb.tile([P, BLOCKS], F32, name="half_steep")
        slot_cols = bank("d2", "slot_cols", [P, P])
        nc.tensor.transpose(slot_cols[:], slot_rows[:], ident[:])
        nc.scalar.activation(neg_th[:], slot_cols[:, 0:BLOCKS], ACT.Copy, scale=-1.0 / P)
        nc.scalar.activation(half_steep[:], slot_cols[:, BLOCKS : 2 * BLOCKS], ACT.Copy, scale=0.5)

        def share(b):
            terms, gap, tanh, al = scratch[b]
            nc.scalar.activation(terms, sum_ps[b][:], ACT.Identity, scale=1.0 / D,
                                 bias=neg_th[:, b : b + 1], accum_out=gap)
            nc.scalar.activation(tanh, gap, ACT.Tanh, scale=half_steep[:, b : b + 1])
            nc.scalar.activation(al, tanh, ACT.Copy, scale=0.25, bias=0.25)
            move_ps.append(bank("s%d" % b, "move_ps%d" % b, [P, PACK, P]))
            width = 2 if b == BLOCKS - 1 else PACK
            for first in range(0, PACK, width):
                ts = slice(first, first + width)
                nc.scalar.activation(move[b][:, ts, :], diff_ps[b][:, ts, :], ACT.Copy, scale=al)
                for t in range(first, first + width):
                    nc.tensor.transpose(move_ps[b][:, t, :], move[b][:, t, :], ident[:])

        gather(0)
        share(0)
        share(1)
        gather(1)
        share(2)
        share(3)

        km = shared.tile([P, CHUNK, PACK], BF16, name="km", align_bytes=64, offset=0)
        q_grouped = shared.tile([P, Q, PACK], BF16, name="q_grouped", align_bytes=64, offset=2 * CHUNK * PACK)
        q_codes = [sb.tile([P, P], U32, name="q_codes%d" % h, tag=tag, align_bytes=64)
                   for h, tag in enumerate(("q_codes0", "move3"))]
        q_scales = [sb.tile([P, P], U8, name="q_scales%d" % h, align_bytes=64) for h in range(HALVES)]
        k_codes = [sb.tile([P, len(SCORE_GROUPS[g]) * P], U32, name="k_codes%d" % g, tag=tag, align_bytes=64)
                   for g, tag in enumerate(("prod1_%d" % LAST_PLANE, "neg_kad1", "prod1_1"))]
        k_scales = [sb.tile([P, len(blocks) * P], U8, name="k_scales%d" % g, align_bytes=64)
                    for g, blocks in enumerate(SCORE_GROUPS)]
        scores = [bank("d3", "scores0", [P, I]), bank("d1", "scores1", [P, I])]

        def by_pairs_out(words):
            return words.rearrange("p (c i) t -> p c t i", i=PAIR)

        def by_pairs_in(rows):
            return rows.rearrange("p t (c i) -> p c t i", i=PAIR)

        def merge(b):
            at = slice(b % 2 * P, (b % 2 + 1) * P)
            nc.vector.tensor_tensor(by_pairs_out(km[:, at, :]), by_pairs_in(move_ps[b][:]),
                                    by_pairs_in(neg_kad[b // 2][:, :, at]), ALU.subtract)

        def quantize_query(h):
            nc.vector.quantize_mx(out=q_codes[h][:].bitcast(FP8X4), scales=q_scales[h][:],
                                  in_=q_grouped[:, h * P : (h + 1) * P, :].rearrange("p q t -> p (q t)"))

        def quantize_keys(g):
            blocks = SCORE_GROUPS[g]
            at = slice(blocks[0] % 2 * P, (blocks[-1] % 2 + 1) * P)
            nc.vector.quantize_mx(out=k_codes[g][:].bitcast(FP8X4), scales=k_scales[g][:],
                                  in_=km[:, at, :].rearrange("p i t -> p (i t)"))

        def score(g, h):
            blocks = SCORE_GROUPS[g]
            nc.tensor.matmul_mx(
                out=scores[h][:, blocks[0] * P : (blocks[-1] + 1) * P],
                lhsT=q_codes[h][:].bitcast(FP8X4),
                lhsT_scale=q_scales[h][:],
                rhs=k_codes[g][:].bitcast(FP8X4),
                rhs_scale=k_scales[g][:],
                start=True,
                stop=True,
            )

        for h in range(HALVES):
            rows_h = slice(h * P, (h + 1) * P)
            nc.vector.tensor_copy(by_pairs_out(q_grouped[:, rows_h, :]), by_pairs_in(q_raw[:, :, rows_h]))
        merge(0)
        merge(1)
        quantize_query(0)
        quantize_keys(0)
        score(0, 0)
        merge(2)
        merge(3)
        quantize_query(1)
        score(0, 1)
        quantize_keys(1)
        quantize_keys(2)
        for h in range(HALVES):
            score(1, h)
            score(2, h)

        for h in range(HALVES):
            neg_max = sb.tile([P, 1], F32, name="neg_max%d" % h)
            nc.vector.tensor_reduce(neg_max[:], scores[h][:], AX.X, ALU.max, negate=True)
            weights = sb.tile([P, I], F32, name="weights%d" % h)
            total = sb.tile([P, 1], F32, name="total%d" % h)
            nc.scalar.activation(weights[:], scores[h][:], ACT.Exp, bias=neg_max[:], accum_out=total[:])
            inverse = sb.tile([P, 1], F32, name="inverse%d" % h)
            nc.vector.reciprocal(inverse[:], total[:])
            result = sb.tile([P, I], F32, name="result%d" % h)
            width = I // 2 if h == HALVES - 1 else I
            for first in range(0, I, width):
                at = slice(first, first + width)
                nc.vector.tensor_scalar(result[:, at], weights[:, at], inverse[:], OUT_SCALE, ALU.mult, ALU.mult)
                nc.sync.dma_start(out[h * P : (h + 1) * P, at], result[:, at])
